import numpy as np
import ml_dtypes


def mxq(x, axis, fmt="e4m3"):
    dtype, down = {"e4m3": (ml_dtypes.float8_e4m3fn, 7), "e5m2": (ml_dtypes.float8_e5m2, 14)}[fmt]
    v = np.moveaxis(np.asarray(x, np.float32).astype(ml_dtypes.bfloat16).astype(np.float64), axis, -1)
    blocks = v.reshape(v.shape[:-1] + (-1, 32))
    amax = np.abs(blocks).max(-1, keepdims=True)
    byte = np.maximum(np.where(amax > 0, np.frexp(amax)[1] - 1 + 127, 0) - down, 1)
    scale = np.exp2(byte - 127.0)
    codes = (blocks / scale).astype(np.float32).astype(dtype).astype(np.float64)
    return np.moveaxis((codes * scale).reshape(v.shape), -1, axis)


WIDE = False


def mx_kscale(k):
    if not WIDE:
        return np.ones(k)
    levels = np.array([10, -10, 5, -5, 0])
    if k % 512:
        return np.exp2(np.random.permutation(np.resize(levels, k // 32))).repeat(32)
    a = np.empty((k // 512, 16))
    for p in range(k // 512):
        a[p, :8] = np.random.permutation(np.resize(levels, 8))
        for g in range(8):
            far = levels[np.abs(levels - a[p, g]) >= 10]
            a[p, g + 8] = far[np.random.randint(len(far))]
    return np.exp2(a.ravel()).repeat(32)


def f64(x):
    return np.asarray(x).astype(np.float64)


def striped(idx):
    return np.tile(np.asarray(idx).reshape(-1, 16).T, (8, 1)).astype(np.uint16)


def unstriped(offs):
    return offs[:16].T.reshape(-1).astype(np.int64)


O, G, T, D, M = 2, 512, 2048, 512, 128


def setup_inputs():
    n = np.random.standard_normal
    s = mx_kscale(D)[:, None]
    grid = lambda x: np.round(x * 32) / 32
    return {
        "cb": (grid(n((O, D, T))) / s).astype(np.float32),
        "w": (n((D, M)) * s / np.sqrt(O * D)).astype(np.float32),
        "norm": np.tile(np.random.randint(32, 129, G) / 64.0, (128, 1)).astype(np.float32),
        "offs": striped(np.random.randint(0, T, O * G)),
    }


def reference(cb, w, norm, offs):
    code = unstriped(offs).reshape(O, G)
    e = sum(f64(cb)[o][:, code[o]] for o in range(O)) * f64(norm)[:1]
    y = mxq(f64(w), 0, "e4m3").T @ mxq(e, 0, "e4m3")
    return y

from contextlib import ExitStack

import concourse.mybir as mybir
from concourse.masks import make_identity

F32 = mybir.dt.float32
BF16 = mybir.dt.bfloat16
U32 = mybir.dt.uint32
U16 = mybir.dt.uint16
U8 = mybir.dt.uint8
FP8X4 = mybir.dt.float8_e4m3fn_x4
MULT = mybir.AluOpType.mult
ADD = mybir.AluOpType.add

P = 128
PACK = 4
BOOKS = 2
CODEWORDS = 2048
COLS = 512
M = 128
FLOPS = 2 * 512 * COLS * M

CHUNKS = ((0, 128), (128, 256), (256, 384), (384, 448), (448, 512))
SPLIT = 448
LAST = PACK - 1


def tile_attend_aq_kernel(tc, cb, w, norm, offs, out):
    nc = tc.nc
    with ExitStack() as ctx:
        keep = ctx.enter_context(tc.tile_pool(name="keep", bufs=1))
        psum = ctx.enter_context(tc.psum_pool(name="psum", bufs=1))

        planes = cb.rearrange("o (p j) c -> o p j c", j=PACK)
        windows = {}

        def load_window(o, j):
            windows[o, j] = keep.tile([P, CODEWORDS], F32, name=f"window{o}{j}")
            nc.sync.dma_start(out=windows[o, j][:], in_=planes[o, :, j, :])

        norm_rows = keep.tile([P, P], F32, name="norm_rows")
        nc.gpsimd.memset(norm_rows[:], 0.0)

        load_window(0, 0)
        nc.sync.dma_start(out=norm_rows[0:4, :], in_=norm[0:1, :].rearrange("o (b j) -> (o b) j", b=4))
        offsets = keep.tile([P, BOOKS * COLS // 16], U16, name="offsets")
        nc.sync.dma_start(offsets[:], offs)
        for j in range(PACK):
            for o in range(BOOKS):
                if (o, j) != (0, 0):
                    load_window(o, j)
        w_raw = keep.tile([P, PACK, M], F32, name="w_raw")
        nc.sync.dma_start(out=w_raw[:], in_=w.rearrange("(p j) m -> p j m", j=PACK))

        ident = keep.tile([P, P], F32, name="ident")
        make_identity(nc, ident[:])
        norm_turned = psum.tile([P, P], F32, name="norm_turned")
        nc.tensor.transpose(norm_turned[:], norm_rows[:], ident[:])
        norm_cols = keep.tile([P, 4], F32, name="norm_cols")
        nc.scalar.copy(out=norm_cols[:], in_=norm_turned[:, 0:4])
        norm_spread = psum.tile([P, COLS], F32, name="norm_spread")
        for b in range(4):
            nc.tensor.transpose(
                norm_spread[:, b * P : (b + 1) * P], norm_cols[:, b : b + 1].to_broadcast([P, P]), ident[:]
            )
        norm_all = keep.tile([P, COLS], F32, name="norm_all")
        nc.scalar.copy(out=norm_all[:], in_=norm_spread[:])

        e_main = keep.tile([P, SPLIT, PACK], BF16, name="e_main", align_bytes=64)
        e_last = keep.tile([P, COLS - SPLIT, PACK], BF16, name="e_last", align_bytes=64)
        e_codes = keep.tile([P, COLS], U32, name="e_codes", align_bytes=64)
        e_scales = keep.tile([P, COLS], U8, name="e_scales", align_bytes=64)
        scaled = {}
        for j in range(PACK):
            for o in range(BOOKS):
                scaled[o, j] = keep.tile([P, COLS], F32, name=f"scaled{o}{j}")
        sums = [keep.tile([P, SPLIT], BF16, name=f"sums{j}") for j in range(PACK)]

        def gather(o, j, lo, hi):
            first = o * COLS // 16
            nc.vector.tensor_tensor(
                scaled[o, j][:, lo:hi],
                windows[o, j][:].indirect(offsets[:, first + lo // 16 : first + hi // 16]),
                norm_all[:, lo:hi],
                MULT,
            )

        def add(j, lo, hi):
            if lo >= SPLIT:
                target = e_last[:, lo - SPLIT : hi - SPLIT, j]
            else:
                target = sums[j][:, lo:hi]
            nc.vector.tensor_tensor(target, scaled[0, j][:, lo:hi], scaled[1, j][:, lo:hi], ADD)

        def interleave(j, lo, hi):
            nc.scalar.copy(out=e_main[:, lo:hi, j], in_=sums[j][:, lo:hi])

        for j in range(LAST):
            gather(0, j, 0, COLS)
            gather(1, j, 0, COLS)
            add(j, 0, SPLIT)
            interleave(j, 0, SPLIT)
            add(j, SPLIT, COLS)
        gather(0, LAST, 0, COLS)

        w_grouped = keep.tile([P, M, PACK], BF16, name="w_grouped", align_bytes=64)
        w_codes = keep.tile([P, M], U32, name="w_codes", align_bytes=64)
        w_scales = keep.tile([P, M], U8, name="w_scales", align_bytes=64)
        nc.scalar.copy(out=w_grouped[:], in_=w_raw[:].rearrange("p j m -> p m j"))

        def quantise(lo, hi):
            if lo >= SPLIT:
                source = e_last[:, lo - SPLIT : hi - SPLIT, :]
            else:
                source = e_main[:, lo:hi, :]
            nc.vector.quantize_mx(
                out=e_codes[:, lo:hi].bitcast(FP8X4),
                scales=e_scales[:, lo:hi],
                in_=source.rearrange("p n j -> p (n j)"),
            )

        banks = {}
        for name, lo, hi in (("y0", 0, 256), ("y1", 256, 448), ("y2", 448, 512)):
            banks[lo, hi] = psum.tile([P, hi - lo], F32, name=name)
        result = keep.tile([P, COLS], F32, name="result")

        def multiply(lo, hi):
            for (blo, bhi), bank in banks.items():
                if blo <= lo and hi <= bhi:
                    nc.tensor.matmul_mx(
                        out=bank[:, lo - blo : hi - blo],
                        lhsT=w_codes[:].bitcast(FP8X4),
                        lhsT_scale=w_scales[:],
                        rhs=e_codes[:, lo:hi].bitcast(FP8X4),
                        rhs_scale=e_scales[:, lo:hi],
                        start=True,
                        stop=True,
                    )

        def finish(lo, hi):
            if hi == COLS:
                nc.vector.tensor_copy(out=result[:, lo:hi], in_=banks[lo, hi][:])
            else:
                nc.scalar.copy(out=result[:, lo:hi], in_=banks[lo, hi][:])
            nc.sync.dma_start(out=out[:, lo:hi], in_=result[:, lo:hi])

        gather(1, LAST, *CHUNKS[0])
        gather(1, LAST, *CHUNKS[1])
        add(LAST, *CHUNKS[0])
        interleave(LAST, *CHUNKS[0])
        gather(1, LAST, *CHUNKS[2])
        add(LAST, *CHUNKS[1])
        interleave(LAST, *CHUNKS[1])
        gather(1, LAST, *CHUNKS[3])
        add(LAST, *CHUNKS[2])
        interleave(LAST, *CHUNKS[2])
        nc.vector.quantize_mx(
            out=w_codes[:].bitcast(FP8X4), scales=w_scales[:], in_=w_grouped[:].rearrange("p m j -> p (m j)")
        )
        gather(1, LAST, *CHUNKS[4])
        add(LAST, *CHUNKS[3])
        interleave(LAST, *CHUNKS[3])
        quantise(*CHUNKS[0])
        multiply(*CHUNKS[0])
        add(LAST, *CHUNKS[4])
        quantise(*CHUNKS[1])
        multiply(*CHUNKS[1])
        finish(0, 256)
        quantise(*CHUNKS[2])
        multiply(*CHUNKS[2])
        quantise(*CHUNKS[3])
        multiply(*CHUNKS[3])
        finish(256, 448)
        quantise(*CHUNKS[4])
        multiply(*CHUNKS[4])
        finish(448, 512)
